import numpy as np
import ml_dtypes


def mxq(x, axis, fmt="e4m3"):
    dtype, down = {"e4m3": (ml_dtypes.float8_e4m3fn, 7), "e5m2": (ml_dtypes.float8_e5m2, 14)}[fmt]
    v = np.moveaxis(np.asarray(x, np.float32).astype(ml_dtypes.bfloat16).astype(np.float64), axis, -1)
    blocks = v.reshape(v.shape[:-1] + (-1, 32))
    amax = np.abs(blocks).max(-1, keepdims=True)
    byte = np.maximum(np.where(amax > 0, np.frexp(amax)[1] - 1 + 127, 0) - down, 1)
    scale = np.exp2(byte - 127.0)
    codes = (blocks / scale).astype(np.float32).astype(dtype).astype(np.float64)
    return np.moveaxis((codes * scale).reshape(v.shape), -1, axis)


WIDE = False


def mx_kscale(k):
    if not WIDE:
        return np.ones(k)
    levels = np.array([10, -10, 5, -5, 0])
    if k % 512:
        return np.exp2(np.random.permutation(np.resize(levels, k // 32))).repeat(32)
    a = np.empty((k // 512, 16))
    for p in range(k // 512):
        a[p, :8] = np.random.permutation(np.resize(levels, 8))
        for g in range(8):
            far = levels[np.abs(levels - a[p, g]) >= 10]
            a[p, g + 8] = far[np.random.randint(len(far))]
    return np.exp2(a.ravel()).repeat(32)


def f64(x):
    return np.asarray(x).astype(np.float64)


def striped(idx):
    return np.tile(np.asarray(idx).reshape(-1, 16).T, (8, 1)).astype(np.uint16)


def unstriped(offs):
    return offs[:16].T.reshape(-1).astype(np.int64)


E2M1 = np.array([0.0, 0.5, 1.0, 1.5, 2.0, 3.0, 4.0, 6.0, -0.0, -0.5, -1.0, -1.5, -2.0, -3.0, -4.0, -6.0])


def pack_weight(w, fmt):
    k, n = w.shape
    w = f64(np.asarray(w, np.float32).astype(ml_dtypes.bfloat16)).reshape(k // 32, 32, n)
    amax = np.abs(w).max(1)
    if fmt == "e4m3":
        byte = np.frexp(amax)[1] - 1 + 127 - 7
    else:
        mant, ex = np.frexp(amax / 6.0)
        byte = np.where(mant > 0.5, ex, ex - 1) + 127
    byte = np.clip(np.where(amax > 0, byte, 1), 1, 254)
    scaled = (w * np.exp2(127.0 - byte)[:, None, :]).reshape(k, n).astype(np.float32)
    by_word = np.ascontiguousarray(scaled.reshape(k // 512, 128, 4, n).transpose(0, 1, 3, 2))
    if fmt == "e4m3":
        words = by_word.astype(ml_dtypes.float8_e4m3fn).view(np.uint8)
    else:
        c = by_word.astype(ml_dtypes.float4_e2m1fn).view(np.uint8) & 0xF
        words = (c[..., 0::2] | (c[..., 1::2] << 4)).reshape(k // 512, 128, 2 * n)
    return np.ascontiguousarray(words), np.ascontiguousarray(byte.astype(np.uint8).reshape(k // 512, 16, n))


def unpack_weight(words, scales, fmt):
    g, _, n = scales.shape
    words = np.ascontiguousarray(words).reshape(g, 128, n, -1)
    if fmt == "e4m3":
        vals = words.view(ml_dtypes.float8_e4m3fn).astype(np.float64)
    else:
        nib = np.empty((g, 128, n, 4), np.uint8)
        nib[..., 0::2] = words & 0xF
        nib[..., 1::2] = words >> 4
        vals = E2M1[nib]
    vals = vals * np.repeat(np.exp2(scales.astype(np.float64) - 127.0), 8, axis=1)[..., None]
    return vals.transpose(0, 1, 3, 2).reshape(g * 512, n)


B, N, T, D, DV, NQ = 1, 1024, 4096, 512, 256, 128


def setup_inputs():
    n = np.random.standard_normal
    idx = np.sort(np.random.permutation(T)[:B * N].reshape(B, N), axis=1).reshape(-1)
    s = mx_kscale(D)[:, None]
    u = np.ones(T)
    u[idx] = mx_kscale(B * N)
    r = np.random.uniform(0.5, 2.0, T)
    k = n((D, T)) / s
    v = n((DV, T)) / (u * r)
    kp = pack_weight(k, "e4m3")
    return {
        "qT": (n((B, D, NQ)) * s * (1.00 / np.sqrt(D))).astype(np.float32),
        "k_words": kp[0],
        "k_scales": kp[1],
        "vT": v.astype(np.float32),
        "vs": np.tile(u * r, (128, 1)).astype(np.float32),
        "offs": striped(idx),
    }


def reference(qT, k_words, k_scales, vT, vs, offs):
    idx = unstriped(offs)
    k = unpack_weight(k_words, k_scales, "e4m3")
    v = f64(vT)
    pick = lambda x: x[:, idx].reshape(x.shape[0], B, N).transpose(1, 0, 2)
    q = f64(qT)
    score = mxq(q, 1, "e4m3").transpose(0, 2, 1) @ pick(k)
    m = score.max(-1, keepdims=True)
    p = np.exp(score - m)
    total = p.sum(-1, keepdims=True)
    w = p * pick(f64(vs))[:, :1, :]
    y = mxq(w, 2, "e4m3") @ mxq(pick(v).transpose(0, 2, 1), 1, "e4m3")
    y = y / total
    return y

@@ -1,0 +1,203 @@
+from contextlib import ExitStack
+
+import concourse.mybir as mybir
+from concourse.masks import make_identity
+
+N, T, D, DV, NQ = 1024, 4096, 512, 256, 128
+FLOPS = 2 * NQ * N * (D + DV)
+BYTES = 4 * D * NQ + D * T + (D // 32) * T + 4 * DV * T + 4 * T + 2 * 128 * (N // 16) + 4 * NQ * DV
+
+F32 = mybir.dt.float32
+BF16 = mybir.dt.bfloat16
+I32 = mybir.dt.int32
+U32 = mybir.dt.uint32
+U16 = mybir.dt.uint16
+U8 = mybir.dt.uint8
+FP8X4 = mybir.dt.float8_e4m3fn_x4
+ALU = mybir.AluOpType
+ACT = mybir.ActivationFunctionType
+
+P = 128
+PACK = 4
+PASS = P * PACK
+PASSES = N // PASS
+LIST_COLS = PASS // 16
+PREFIX = T - N + PASS
+VS_ROW = 16
+V0_CHUNKS = [(0, 1024), (1024, 2048), (2048, 3072), (3072, PREFIX), (PREFIX, T)]
+
+
+def tile_attend_soft_srt_kernel(tc, qT, k_words, k_scales, vT, vs, offs, out):
+    nc = tc.nc
+    with ExitStack() as ctx:
+        keep = ctx.enter_context(tc.tile_pool(name="keep", bufs=1))
+        psum = ctx.enter_context(tc.psum_pool(name="psum", bufs=1))
+
+        offsets = keep.tile([P, N // 16], U16, name="offsets")
+        nc.sync.dma_start(offsets[:], offs)
+
+        def slots(g):
+            return offsets[:, g * LIST_COLS : (g + 1) * LIST_COLS]
+
+        q_raw = keep.tile([P, PACK, NQ], F32, name="q_raw")
+        nc.sync.dma_start(q_raw[:], qT[0].rearrange("(p j) q -> p j q", j=PACK))
+
+        key_pool = keep.tile([P, T], U32, name="key_pool", tag="then_v1")
+        key_src = k_words[0].rearrange("p n t -> p (n t)").bitcast(I32)
+        nc.sync.dma_start(key_pool[:, :PREFIX].bitcast(I32), key_src[:, :PREFIX])
+        nc.sync.dma_start(key_pool[:, PREFIX:].bitcast(I32), key_src[:, PREFIX:])
+
+        kscale_pool = keep.tile([P, T], U8, name="kscale_pool", tag="then_keys", align_bytes=64)
+        nc.vector.memset(kscale_pool[:].bitcast(I32), 0)
+        for quad in range(4):
+            nc.scalar.dma_start(
+                kscale_pool[32 * quad : 32 * quad + 4, :].bitcast(I32),
+                k_scales[0, 4 * quad : 4 * quad + 4, :].bitcast(I32),
+            )
+
+        vs_pool = keep.tile([P, T], F32, name="vs_pool")
+        nc.vector.memset(vs_pool[:].bitcast(I32), 0)
+        nc.sync.dma_start(vs_pool[VS_ROW : VS_ROW + 1, :], vs[0:1, :])
+
+        ident = keep.tile([P, P], F32, name="ident")
+        make_identity(nc, ident[:])
+
+        q_bf = keep.tile([P, NQ, PACK], BF16, name="q_bf", tag="then_v0", align_bytes=64)
+        nc.scalar.activation(q_bf[:], q_raw[:].rearrange("p j q -> p q j"), ACT.Copy)
+        q_codes = keep.tile([P, NQ], U32, name="q_codes", align_bytes=64)
+        q_scales = keep.tile([P, NQ], U8, name="q_scales", align_bytes=64)
+        nc.vector.quantize_mx(out=q_codes[:].bitcast(FP8X4), scales=q_scales[:], in_=q_bf[:].rearrange("p q j -> p (q j)"))
+
+        kscales = keep.tile([P, N], U8, name="kscales", align_bytes=64)
+        nc.vector.tensor_copy(kscales[:], kscale_pool[:].indirect(offsets[:]))
+
+        v_pool = [
+            keep.tile([P, T], F32, name="v_pool0", tag="then_v0", align_bytes=64),
+            keep.tile([P, T], F32, name="v_pool1", tag="then_v1"),
+        ]
+        v0_prefix = keep.tile([P, PREFIX], BF16, name="v0_prefix")
+        for c0, c1 in V0_CHUNKS:
+            nc.sync.dma_start(v_pool[0][:, c0:c1], vT[0:P, c0:c1])
+        nc.sync.dma_start(v_pool[1][:, :PREFIX], vT[P : 2 * P, :PREFIX])
+        nc.sync.dma_start(v_pool[1][:, PREFIX:], vT[P : 2 * P, PREFIX:])
+
+        vs_cols = keep.tile([P, PASSES, PACK], F32, name="vs_cols")
+
+        def token_scales(g):
+            vs_row = keep.tile([P, PASS], F32, name=f"vs_row{g}")
+            nc.vector.tensor_copy(vs_row[:], vs_pool[:].indirect(slots(g)))
+            turned = psum.tile([P, PACK, P], F32, name="turned", tag="turned", bufs=2)
+            for t in range(PACK):
+                nc.tensor.transpose(turned[:, t, :], vs_row[:, t:PASS:PACK], ident[:])
+            nc.scalar.copy(vs_cols[:, g, :], turned[:, :, VS_ROW])
+
+        keys = keep.tile([P, N], U32, name="keys", tag="then_keys", align_bytes=64)
+        scores = [psum.tile([P, PASS], F32, name=f"scores{g}") for g in range(PASSES)]
+        for g in range(PASSES):
+            cols = slice(g * PASS, (g + 1) * PASS)
+            window = key_pool[:, :PREFIX] if g == 0 else key_pool[:]
+            nc.vector.tensor_copy(keys[:, cols], window.indirect(slots(g)))
+            nc.tensor.matmul_mx(
+                out=scores[g][:], lhsT=q_codes[:].bitcast(FP8X4), lhsT_scale=q_scales[:],
+                rhs=keys[:, cols].bitcast(FP8X4), rhs_scale=kscales[:, cols], start=True, stop=True,
+            )
+        neg_max0 = keep.tile([P, 1], F32, name="neg_max0")
+        neg_max = keep.tile([P, 1], F32, name="neg_max")
+        neg_scores = keep.tile([P, PASS], F32, name="neg_scores")
+        nc.vector.tensor_reduce(neg_max0[:], scores[0][:], mybir.AxisListType.X, ALU.max, negate=True)
+        nc.vector.tensor_scalar(neg_scores[:], scores[1][:], -1.0, neg_max0[:], ALU.mult, ALU.min, accum_out=neg_max[:])
+
+        for c0, c1 in V0_CHUNKS[:2]:
+            nc.scalar.copy(v0_prefix[:, c0:c1], v_pool[0][:, c0:c1])
+        token_scales(0)
+        token_scales(1)
+
+        sums = keep.tile([P, PASSES], F32, name="sums")
+        w_bf = keep.tile([P, PASSES, NQ, PACK], BF16, name="w_bf", align_bytes=64)
+        p_turned = []
+        for g in range(PASSES):
+            p = keep.tile([P, PACK, P], F32, name=f"p{g}")
+            if g == 0:
+                nc.scalar.activation(p[:], scores[g][:].rearrange("q (s t) -> q t s", t=PACK), ACT.Exp,
+                                     bias=neg_max[:], scale=1.0, accum_out=sums[:, g : g + 1])
+            else:
+                nc.scalar.activation(p[:], neg_scores[:].rearrange("q (s t) -> q t s", t=PACK), ACT.Exp,
+                                     bias=neg_max[:], scale=-1.0, accum_out=sums[:, g : g + 1])
+            turned = psum.tile([P, PACK, P], F32, name="turned", tag="turned", bufs=2)
+            for t in range(PACK):
+                nc.tensor.transpose(turned[:, t, :], p[:, t, :], ident[:])
+            p_turned.append(turned)
+
+        v_bf = [keep.tile([P, PASSES, P, PACK], BF16, name=f"v_bf{h}", align_bytes=64) for h in range(2)]
+        v_codes = [keep.tile([P, PASSES, P], U32, name=f"v_codes{h}", align_bytes=64) for h in range(2)]
+        v_scales = [keep.tile([P, PASSES, P], U8, name=f"v_scales{h}", align_bytes=64) for h in range(2)]
+
+        def values_bf16(h, g):
+            picked = keep.tile([P, PASS], BF16, name=f"picked{h}{g}")
+            if (h, g) == (0, 0):
+                nc.scalar.activation(picked[:], v0_prefix[:].indirect(slots(g)), ACT.Copy)
+            else:
+                nc.vector.tensor_copy(picked[:], v_pool[h][:].indirect(slots(g)))
+            pairs = picked[:].bitcast(F32)
+            v_turned = psum.tile([P, 2, P], F32, name="v_turned", tag="v_turned", bufs=2)
+            for u in range(2):
+                nc.tensor.transpose(v_turned[:, u, :], pairs[:, u : PASS // 2 : 2], ident[:])
+            nc.scalar.copy(v_bf[h][:, g, :, :].bitcast(F32), v_turned[:].rearrange("s u e -> s e u"))
+
+        def values_f32(h, g):
+            picked = keep.tile([P, PASS], F32, name=f"picked{h}{g}")
+            nc.vector.tensor_copy(picked[:], v_pool[h][:, :PREFIX].indirect(slots(g)))
+            v_turned = psum.tile([P, PACK, P], F32, name="v_turned", tag="v_turned", bufs=2)
+            for t in range(PACK):
+                nc.tensor.transpose(v_turned[:, t, :], picked[:, t:PASS:PACK], ident[:])
+            nc.scalar.copy(v_bf[h][:, g, :, :], v_turned[:].rearrange("s t e -> s e t"))
+
+        for c0, c1 in V0_CHUNKS[2:4]:
+            nc.scalar.copy(v0_prefix[:, c0:c1], v_pool[0][:, c0:c1])
+        values_bf16(0, 0)
+        values_bf16(0, 1)
+
+        for g in range(PASSES):
+            nc.vector.tensor_tensor(
+                w_bf[:, g, :, :], p_turned[g][:].rearrange("s t q -> s q t"),
+                vs_cols[:, g, :].unsqueeze(1).to_broadcast([P, NQ, PACK]), ALU.mult,
+            )
+        w_codes = keep.tile([P, PASSES, NQ], U32, name="w_codes", align_bytes=64)
+        w_scales = keep.tile([P, PASSES, NQ], U8, name="w_scales", align_bytes=64)
+        total = keep.tile([P, 1], F32, name="total")
+        inv_total = keep.tile([P, 1], F32, name="inv_total")
+        nc.vector.quantize_mx(
+            out=v_codes[0][:].rearrange("p g e -> p (g e)").bitcast(FP8X4),
+            scales=v_scales[0][:].rearrange("p g e -> p (g e)"),
+            in_=v_bf[0][:].rearrange("p g e t -> p (g e t)"),
+        )
+        nc.vector.tensor_tensor(total[:], sums[:, 0:1], sums[:, 1:2], ALU.add)
+        nc.vector.quantize_mx(
+            out=w_codes[:].rearrange("p g q -> p (g q)").bitcast(FP8X4),
+            scales=w_scales[:].rearrange("p g q -> p (g q)"),
+            in_=w_bf[:].rearrange("p g q t -> p (g q t)"),
+        )
+        nc.vector.reciprocal(inv_total[:], total[:])
+
+        def product(h):
+            acc = psum.tile([P, P], F32, name=f"acc{h}")
+            for g in range(PASSES):
+                nc.tensor.matmul_mx(
+                    out=acc[:], lhsT=w_codes[:, g, :].bitcast(FP8X4), lhsT_scale=w_scales[:, g, :],
+                    rhs=v_codes[h][:, g, :].bitcast(FP8X4), rhs_scale=v_scales[h][:, g, :],
+                    start=(g == 0), stop=(g == PASSES - 1),
+                )
+            result = keep.tile([P, P], F32, name=f"result{h}")
+            nc.scalar.activation(result[:], acc[:], ACT.Copy, scale=inv_total[:])
+            nc.sync.dma_start(out[0, :, h * P : (h + 1) * P], result[:])
+
+        product(0)
+
+        values_f32(1, 0)
+        values_bf16(1, 1)
+        for g in range(PASSES):
+            nc.vector.quantize_mx(
+                out=v_codes[1][:, g, :].bitcast(FP8X4), scales=v_scales[1][:, g, :],
+                in_=v_bf[1][:, g, :, :].rearrange("p e t -> p (e t)"),
+            )
+        product(1)

@@ -22,9 +22,10 @@ PACK = 4
 PASS = P * PACK
 PASSES = N // PASS
 LIST_COLS = PASS // 16
-PREFIX = T - N + PASS
 VS_ROW = 16
-V0_CHUNKS = [(0, 1024), (1024, 2048), (2048, 3072), (3072, PREFIX), (PREFIX, T)]
+ZERO_SPLIT = 3072
+PREFIX = T - N + PASS
+V0_CHUNKS = ((0, 1024), (1024, 2048), (2048, 2560), (2560, T))
 
 
 def tile_attend_soft_srt_kernel(tc, qT, k_words, k_scales, vT, vs, offs, out):
@@ -33,171 +34,161 @@ def tile_attend_soft_srt_kernel(tc, qT, k_words, k_scales, vT, vs, offs, out):
         keep = ctx.enter_context(tc.tile_pool(name="keep", bufs=1))
         psum = ctx.enter_context(tc.psum_pool(name="psum", bufs=1))
 
+        def sbuf(shape, dtype, name, tag=None):
+            return keep.tile(shape, dtype, name=name, tag=tag or name, align_bytes=64)
+
         offsets = keep.tile([P, N // 16], U16, name="offsets")
         nc.sync.dma_start(offsets[:], offs)
 
         def slots(g):
             return offsets[:, g * LIST_COLS : (g + 1) * LIST_COLS]
 
-        q_raw = keep.tile([P, PACK, NQ], F32, name="q_raw")
+        q_raw = sbuf([P, PACK, NQ], F32, "q_raw")
         nc.sync.dma_start(q_raw[:], qT[0].rearrange("(p j) q -> p j q", j=PACK))
 
-        key_pool = keep.tile([P, T], U32, name="key_pool", tag="then_v1")
+        def load_v0(i, tag=None):
+            c0, c1 = V0_CHUNKS[i]
+            chunk = sbuf([P, c1 - c0], F32, f"v0_chunk{i}", tag=tag)
+            nc.sync.dma_start(chunk[:], vT[0:P, c0:c1])
+            return chunk
+
+        v0_chunks = [load_v0(i) for i in range(len(V0_CHUNKS) - 1)]
+
+        kscale_pool = sbuf([P, T], U8, "kscale_pool")
+        nc.gpsimd.memset(kscale_pool[:].bitcast(I32), 0)
+        for quad in range(4):
+            nc.sync.dma_start(
+                kscale_pool[32 * quad : 32 * quad + 4, :].bitcast(I32),
+                k_scales[0, 4 * quad : 4 * quad + 4, :].bitcast(I32),
+            )
+        vs_pool = sbuf([P, T], F32, "vs_pool")
+        nc.vector.memset(vs_pool[:, :ZERO_SPLIT].bitcast(I32), 0)
+        nc.gpsimd.memset(vs_pool[:, ZERO_SPLIT:].bitcast(I32), 0)
+        nc.sync.dma_start(vs_pool[VS_ROW : VS_ROW + 1, :], vs[0:1, :])
+        ident = sbuf([P, P], F32, "ident")
+        make_identity(nc, ident[:])
+
+        q_bf = sbuf([P, NQ, PACK], BF16, "q_bf")
+        nc.scalar.activation(q_bf[:], q_raw[:].rearrange("p j q -> p q j"), ACT.Copy)
+        q_codes = sbuf([P, NQ], U32, "q_codes")
+        q_scales = sbuf([P, NQ], U8, "q_scales")
+        nc.vector.quantize_mx(
+            out=q_codes[:].bitcast(FP8X4), scales=q_scales[:], in_=q_bf[:].rearrange("p q j -> p (q j)")
+        )
+
+        v0_chunks.append(load_v0(len(V0_CHUNKS) - 1, tag="q_raw"))
+        v0_pool_bf = sbuf([P, T], BF16, "v0_pool_bf")
+        for (c0, c1), chunk in zip(V0_CHUNKS, v0_chunks):
+            nc.scalar.copy(v0_pool_bf[:, c0:c1], chunk[:])
+
+        key_pool = sbuf([P, T], U32, "key_pool", tag="v0_chunk0")
         key_src = k_words[0].rearrange("p n t -> p (n t)").bitcast(I32)
         nc.sync.dma_start(key_pool[:, :PREFIX].bitcast(I32), key_src[:, :PREFIX])
         nc.sync.dma_start(key_pool[:, PREFIX:].bitcast(I32), key_src[:, PREFIX:])
 
-        kscale_pool = keep.tile([P, T], U8, name="kscale_pool", tag="then_keys", align_bytes=64)
-        nc.vector.memset(kscale_pool[:].bitcast(I32), 0)
-        for quad in range(4):
-            nc.scalar.dma_start(
-                kscale_pool[32 * quad : 32 * quad + 4, :].bitcast(I32),
-                k_scales[0, 4 * quad : 4 * quad + 4, :].bitcast(I32),
-            )
-
-        vs_pool = keep.tile([P, T], F32, name="vs_pool")
-        nc.vector.memset(vs_pool[:].bitcast(I32), 0)
-        nc.sync.dma_start(vs_pool[VS_ROW : VS_ROW + 1, :], vs[0:1, :])
-
-        ident = keep.tile([P, P], F32, name="ident")
-        make_identity(nc, ident[:])
-
-        q_bf = keep.tile([P, NQ, PACK], BF16, name="q_bf", tag="then_v0", align_bytes=64)
-        nc.scalar.activation(q_bf[:], q_raw[:].rearrange("p j q -> p q j"), ACT.Copy)
-        q_codes = keep.tile([P, NQ], U32, name="q_codes", align_bytes=64)
-        q_scales = keep.tile([P, NQ], U8, name="q_scales", align_bytes=64)
-        nc.vector.quantize_mx(out=q_codes[:].bitcast(FP8X4), scales=q_scales[:], in_=q_bf[:].rearrange("p q j -> p (q j)"))
-
-        kscales = keep.tile([P, N], U8, name="kscales", align_bytes=64)
+        kscales = sbuf([P, N], U8, "kscales", tag="q_bf")
         nc.vector.tensor_copy(kscales[:], kscale_pool[:].indirect(offsets[:]))
 
-        v_pool = [
-            keep.tile([P, T], F32, name="v_pool0", tag="then_v0", align_bytes=64),
-            keep.tile([P, T], F32, name="v_pool1", tag="then_v1"),
-        ]
-        v0_prefix = keep.tile([P, PREFIX], BF16, name="v0_prefix")
-        for c0, c1 in V0_CHUNKS:
-            nc.sync.dma_start(v_pool[0][:, c0:c1], vT[0:P, c0:c1])
-        nc.sync.dma_start(v_pool[1][:, :PREFIX], vT[P : 2 * P, :PREFIX])
-        nc.sync.dma_start(v_pool[1][:, PREFIX:], vT[P : 2 * P, PREFIX:])
+        v1_pool = sbuf([P, T], F32, "v1_pool", tag="kscale_pool")
+        nc.sync.dma_start(v1_pool[:], vT[P : 2 * P, :])
 
-        vs_cols = keep.tile([P, PASSES, PACK], F32, name="vs_cols")
+        vs_rows = sbuf([P, PASSES, PASS], F32, "vs_rows")
+        for g in range(PASSES):
+            nc.vector.tensor_copy(vs_rows[:, g, :], vs_pool[:].indirect(slots(g)))
 
-        def token_scales(g):
-            vs_row = keep.tile([P, PASS], F32, name=f"vs_row{g}")
-            nc.vector.tensor_copy(vs_row[:], vs_pool[:].indirect(slots(g)))
-            turned = psum.tile([P, PACK, P], F32, name="turned", tag="turned", bufs=2)
+        def turn_places(dealt, tag):
+            turned = psum.tile([P, PACK, P], F32, name="turned_places", tag=tag)
             for t in range(PACK):
-                nc.tensor.transpose(turned[:, t, :], vs_row[:, t:PASS:PACK], ident[:])
-            nc.scalar.copy(vs_cols[:, g, :], turned[:, :, VS_ROW])
+                nc.tensor.transpose(turned[:, t, :], dealt[:, t, :], ident[:])
+            return turned
 
-        keys = keep.tile([P, N], U32, name="keys", tag="then_keys", align_bytes=64)
-        scores = [psum.tile([P, PASS], F32, name=f"scores{g}") for g in range(PASSES)]
+        v0_picked = sbuf([P, N], BF16, "v0_picked")
+        nc.scalar.activation(v0_picked[:], v0_pool_bf[:].indirect(offsets[:]), ACT.Copy)
+
+        vs_turned = [
+            turn_places(vs_rows[:, g, :].rearrange("m (s t) -> m t s", t=PACK), f"spare{g}") for g in range(PASSES)
+        ]
+
+        keys = sbuf([P, N], U32, "keys", tag="vs_pool")
+        scores = psum.tile([P, PASSES, PASS], F32, name="scores", tag="scores")
         for g in range(PASSES):
             cols = slice(g * PASS, (g + 1) * PASS)
             window = key_pool[:, :PREFIX] if g == 0 else key_pool[:]
             nc.vector.tensor_copy(keys[:, cols], window.indirect(slots(g)))
             nc.tensor.matmul_mx(
-                out=scores[g][:], lhsT=q_codes[:].bitcast(FP8X4), lhsT_scale=q_scales[:],
+                out=scores[:, g, :], lhsT=q_codes[:].bitcast(FP8X4), lhsT_scale=q_scales[:],
                 rhs=keys[:, cols].bitcast(FP8X4), rhs_scale=kscales[:, cols], start=True, stop=True,
             )
-        neg_max0 = keep.tile([P, 1], F32, name="neg_max0")
-        neg_max = keep.tile([P, 1], F32, name="neg_max")
-        neg_scores = keep.tile([P, PASS], F32, name="neg_scores")
-        nc.vector.tensor_reduce(neg_max0[:], scores[0][:], mybir.AxisListType.X, ALU.max, negate=True)
-        nc.vector.tensor_scalar(neg_scores[:], scores[1][:], -1.0, neg_max0[:], ALU.mult, ALU.min, accum_out=neg_max[:])
+        neg_max0 = sbuf([P, 1], F32, "neg_max0")
+        neg_max = sbuf([P, 1], F32, "neg_max")
+        neg_scores = sbuf([P, PASS], F32, "neg_scores")
+        nc.vector.tensor_reduce(neg_max0[:], scores[:, 0, :], mybir.AxisListType.X, ALU.max, negate=True)
+        nc.vector.tensor_scalar(neg_scores[:], scores[:, 1, :], -1.0, neg_max0[:], ALU.mult, ALU.min, accum_out=neg_max[:])
 
-        for c0, c1 in V0_CHUNKS[:2]:
-            nc.scalar.copy(v0_prefix[:, c0:c1], v_pool[0][:, c0:c1])
-        token_scales(0)
-        token_scales(1)
+        vs_cols = sbuf([P, PASSES, PACK], F32, "vs_cols", tag="vs_pool")
+        for g in range(PASSES):
+            nc.scalar.copy(vs_cols[:, g, :], vs_turned[g][:, :, VS_ROW])
 
-        sums = keep.tile([P, PASSES], F32, name="sums")
-        w_bf = keep.tile([P, PASSES, NQ, PACK], BF16, name="w_bf", align_bytes=64)
+        sums = sbuf([P, PASSES], F32, "sums")
         p_turned = []
         for g in range(PASSES):
-            p = keep.tile([P, PACK, P], F32, name=f"p{g}")
-            if g == 0:
-                nc.scalar.activation(p[:], scores[g][:].rearrange("q (s t) -> q t s", t=PACK), ACT.Exp,
-                                     bias=neg_max[:], scale=1.0, accum_out=sums[:, g : g + 1])
-            else:
-                nc.scalar.activation(p[:], neg_scores[:].rearrange("q (s t) -> q t s", t=PACK), ACT.Exp,
-                                     bias=neg_max[:], scale=-1.0, accum_out=sums[:, g : g + 1])
-            turned = psum.tile([P, PACK, P], F32, name="turned", tag="turned", bufs=2)
-            for t in range(PACK):
-                nc.tensor.transpose(turned[:, t, :], p[:, t, :], ident[:])
-            p_turned.append(turned)
+            p = sbuf([P, PACK, P], F32, f"p{g}")
+            nc.scalar.activation(
+                p[:], scores[:, g, :].rearrange("q (s t) -> q t s", t=PACK), ACT.Exp,
+                bias=neg_max[:], accum_out=sums[:, g : g + 1],
+            )
+            p_turned.append(turn_places(p[:], f"turn{g}"))
 
-        v_bf = [keep.tile([P, PASSES, P, PACK], BF16, name=f"v_bf{h}", align_bytes=64) for h in range(2)]
-        v_codes = [keep.tile([P, PASSES, P], U32, name=f"v_codes{h}", align_bytes=64) for h in range(2)]
-        v_scales = [keep.tile([P, PASSES, P], U8, name=f"v_scales{h}", align_bytes=64) for h in range(2)]
+        v_bf = sbuf([P, PASSES, DV, PACK], BF16, "v_bf")
 
-        def values_bf16(h, g):
-            picked = keep.tile([P, PASS], BF16, name=f"picked{h}{g}")
-            if (h, g) == (0, 0):
-                nc.scalar.activation(picked[:], v0_prefix[:].indirect(slots(g)), ACT.Copy)
-            else:
-                nc.vector.tensor_copy(picked[:], v_pool[h][:].indirect(slots(g)))
-            pairs = picked[:].bitcast(F32)
-            v_turned = psum.tile([P, 2, P], F32, name="v_turned", tag="v_turned", bufs=2)
+        def turn_values(picked, turned, g, h):
+            pairs = picked[:, g * PASS : (g + 1) * PASS].bitcast(F32)
             for u in range(2):
-                nc.tensor.transpose(v_turned[:, u, :], pairs[:, u : PASS // 2 : 2], ident[:])
-            nc.scalar.copy(v_bf[h][:, g, :, :].bitcast(F32), v_turned[:].rearrange("s u e -> s e u"))
+                nc.tensor.transpose(turned[:, u * P : (u + 1) * P], pairs[:, u : PASS // 2 : 2], ident[:])
+            nc.scalar.copy(
+                v_bf[:, g, h * P : (h + 1) * P, :].bitcast(F32),
+                turned[:, : 2 * P].rearrange("s (u e) -> s e u", u=2),
+            )
 
-        def values_f32(h, g):
-            picked = keep.tile([P, PASS], F32, name=f"picked{h}{g}")
-            nc.vector.tensor_copy(picked[:], v_pool[h][:, :PREFIX].indirect(slots(g)))
-            v_turned = psum.tile([P, PACK, P], F32, name="v_turned", tag="v_turned", bufs=2)
-            for t in range(PACK):
-                nc.tensor.transpose(v_turned[:, t, :], picked[:, t:PASS:PACK], ident[:])
-            nc.scalar.copy(v_bf[h][:, g, :, :], v_turned[:].rearrange("s t e -> s e t"))
+        for g in range(PASSES):
+            v0_turned = psum.tile([P, 2 * P], F32, name="v0_turned", tag=f"spare{g}")
+            turn_values(v0_picked, v0_turned[:], g, 0)
+        v1_picked = sbuf([P, N], BF16, "v1_picked", tag="neg_max0")
+        v1_turned = psum.tile([P, PASSES, PASS], F32, name="v1_turned", tag="scores")
+        for g in range(PASSES):
+            nc.vector.tensor_copy(v1_picked[:, g * PASS : (g + 1) * PASS], v1_pool[:].indirect(slots(g)))
+            turn_values(v1_picked, v1_turned[:, g, :], g, 1)
 
-        for c0, c1 in V0_CHUNKS[2:4]:
-            nc.scalar.copy(v0_prefix[:, c0:c1], v_pool[0][:, c0:c1])
-        values_bf16(0, 0)
-        values_bf16(0, 1)
-
+        w_bf = sbuf([P, PASSES, NQ, PACK], BF16, "w_bf", tag="kscale_pool")
         for g in range(PASSES):
             nc.vector.tensor_tensor(
                 w_bf[:, g, :, :], p_turned[g][:].rearrange("s t q -> s q t"),
                 vs_cols[:, g, :].unsqueeze(1).to_broadcast([P, NQ, PACK]), ALU.mult,
             )
-        w_codes = keep.tile([P, PASSES, NQ], U32, name="w_codes", align_bytes=64)
-        w_scales = keep.tile([P, PASSES, NQ], U8, name="w_scales", align_bytes=64)
-        total = keep.tile([P, 1], F32, name="total")
-        inv_total = keep.tile([P, 1], F32, name="inv_total")
-        nc.vector.quantize_mx(
-            out=v_codes[0][:].rearrange("p g e -> p (g e)").bitcast(FP8X4),
-            scales=v_scales[0][:].rearrange("p g e -> p (g e)"),
-            in_=v_bf[0][:].rearrange("p g e t -> p (g e t)"),
-        )
+        total = sbuf([P, 1], F32, "total")
         nc.vector.tensor_tensor(total[:], sums[:, 0:1], sums[:, 1:2], ALU.add)
+        w_codes = sbuf([P, PASSES, NQ], U32, "w_codes")
+        w_scales = sbuf([P, PASSES, NQ], U8, "w_scales")
         nc.vector.quantize_mx(
             out=w_codes[:].rearrange("p g q -> p (g q)").bitcast(FP8X4),
             scales=w_scales[:].rearrange("p g q -> p (g q)"),
             in_=w_bf[:].rearrange("p g q t -> p (g q t)"),
         )
+        v_codes = sbuf([P, PASSES, DV], U32, "v_codes")
+        v_scales = sbuf([P, PASSES, DV], U8, "v_scales")
+        inv_total = sbuf([P, 1], F32, "inv_total")
         nc.vector.reciprocal(inv_total[:], total[:])
-
-        def product(h):
-            acc = psum.tile([P, P], F32, name=f"acc{h}")
-            for g in range(PASSES):
-                nc.tensor.matmul_mx(
-                    out=acc[:], lhsT=w_codes[:, g, :].bitcast(FP8X4), lhsT_scale=w_scales[:, g, :],
-                    rhs=v_codes[h][:, g, :].bitcast(FP8X4), rhs_scale=v_scales[h][:, g, :],
-                    start=(g == 0), stop=(g == PASSES - 1),
-                )
-            result = keep.tile([P, P], F32, name=f"result{h}")
-            nc.scalar.activation(result[:], acc[:], ACT.Copy, scale=inv_total[:])
-            nc.sync.dma_start(out[0, :, h * P : (h + 1) * P], result[:])
-
-        product(0)
-
-        values_f32(1, 0)
-        values_bf16(1, 1)
+        acc = psum.tile([P, DV], F32, name="acc", tag="spare0")
         for g in range(PASSES):
             nc.vector.quantize_mx(
-                out=v_codes[1][:, g, :].bitcast(FP8X4), scales=v_scales[1][:, g, :],
-                in_=v_bf[1][:, g, :, :].rearrange("p e t -> p (e t)"),
+                out=v_codes[:, g, :].bitcast(FP8X4), scales=v_scales[:, g, :],
+                in_=v_bf[:, g, :, :].rearrange("p e t -> p (e t)"),
             )
-        product(1)
+            nc.tensor.matmul_mx(
+                out=acc[:], lhsT=w_codes[:, g, :].bitcast(FP8X4), lhsT_scale=w_scales[:, g, :],
+                rhs=v_codes[:, g, :].bitcast(FP8X4), rhs_scale=v_scales[:, g, :],
+                start=(g == 0), stop=(g == PASSES - 1),
+            )
+        result = sbuf([P, DV], F32, "result")
+        nc.vector.tensor_scalar(result[:], acc[:], inv_total[:], None, ALU.mult)
+        nc.sync.dma_start(out[0], result[:])

@@ -92,9 +92,8 @@ def tile_attend_soft_srt_kernel(tc, qT, k_words, k_scales, vT, vs, offs, out):
         v1_pool = sbuf([P, T], F32, "v1_pool", tag="kscale_pool")
         nc.sync.dma_start(v1_pool[:], vT[P : 2 * P, :])
 
-        vs_rows = sbuf([P, PASSES, PASS], F32, "vs_rows")
-        for g in range(PASSES):
-            nc.vector.tensor_copy(vs_rows[:, g, :], vs_pool[:].indirect(slots(g)))
+        vs_rows = sbuf([P, N], F32, "vs_rows")
+        nc.vector.tensor_copy(vs_rows[:], vs_pool[:].indirect(offsets[:]))
 
         def turn_places(dealt, tag):
             turned = psum.tile([P, PACK, P], F32, name="turned_places", tag=tag)
@@ -102,12 +101,27 @@ def tile_attend_soft_srt_kernel(tc, qT, k_words, k_scales, vT, vs, offs, out):
                 nc.tensor.transpose(turned[:, t, :], dealt[:, t, :], ident[:])
             return turned
 
-        v0_picked = sbuf([P, N], BF16, "v0_picked")
-        nc.scalar.activation(v0_picked[:], v0_pool_bf[:].indirect(offsets[:]), ACT.Copy)
+        vs_dealt = sbuf([P, PASSES, PACK, P], F32, "vs_dealt")
+        nc.vector.tensor_copy(vs_dealt[:], vs_rows[:].rearrange("m (g s t) -> m g t s", g=PASSES, t=PACK))
+        vs_turned = [turn_places(vs_dealt[:, g, :, :], f"spare{g}") for g in range(PASSES)]
 
-        vs_turned = [
-            turn_places(vs_rows[:, g, :].rearrange("m (s t) -> m t s", t=PACK), f"spare{g}") for g in range(PASSES)
-        ]
+        v_bf = [sbuf([P, PASSES, P, PACK], BF16, f"v_bf{h}") for h in range(2)]
+
+        def turn_values(picked, turned, laid):
+            pairs = picked.bitcast(F32)
+            for u in range(2):
+                nc.tensor.transpose(turned[:, u * P : (u + 1) * P], pairs[:, u : PASS // 2 : 2], ident[:])
+            nc.scalar.copy(laid.bitcast(F32), turned[:, : 2 * P].rearrange("s (u e) -> s e u", u=2))
+
+        for g in range(PASSES):
+            v0_picked = sbuf([P, PASS], BF16, f"v0_picked{g}")
+            nc.scalar.activation(v0_picked[:], v0_pool_bf[:].indirect(slots(g)), ACT.Copy)
+            v0_turned = psum.tile([P, 2 * P], F32, name="v0_turned", tag=f"turn{g}")
+            turn_values(v0_picked[:], v0_turned[:], v_bf[0][:, g, :, :])
+
+        vs_cols = sbuf([P, PASSES, PACK], F32, "vs_cols", tag="v0_pool_bf")
+        for g in range(PASSES):
+            nc.scalar.copy(vs_cols[:, g, :], vs_turned[g][:, :, VS_ROW])
 
         keys = sbuf([P, N], U32, "keys", tag="vs_pool")
         scores = psum.tile([P, PASSES, PASS], F32, name="scores", tag="scores")
@@ -123,11 +137,20 @@ def tile_attend_soft_srt_kernel(tc, qT, k_words, k_scales, vT, vs, offs, out):
         neg_max = sbuf([P, 1], F32, "neg_max")
         neg_scores = sbuf([P, PASS], F32, "neg_scores")
         nc.vector.tensor_reduce(neg_max0[:], scores[:, 0, :], mybir.AxisListType.X, ALU.max, negate=True)
-        nc.vector.tensor_scalar(neg_scores[:], scores[:, 1, :], -1.0, neg_max0[:], ALU.mult, ALU.min, accum_out=neg_max[:])
 
-        vs_cols = sbuf([P, PASSES, PACK], F32, "vs_cols", tag="vs_pool")
+        v_codes = sbuf([P, PASSES, DV], U32, "v_codes", tag="v0_chunk0")
+        v_scales = sbuf([P, PASSES, DV], U8, "v_scales")
+
+        def quantise_values(g, h):
+            nc.vector.quantize_mx(
+                out=v_codes[:, g, h * P : (h + 1) * P].bitcast(FP8X4),
+                scales=v_scales[:, g, h * P : (h + 1) * P],
+                in_=v_bf[h][:, g, :, :].rearrange("p e t -> p (e t)"),
+            )
+
         for g in range(PASSES):
-            nc.scalar.copy(vs_cols[:, g, :], vs_turned[g][:, :, VS_ROW])
+            quantise_values(g, 0)
+        nc.vector.tensor_scalar(neg_scores[:], scores[:, 1, :], -1.0, neg_max0[:], ALU.mult, ALU.min, accum_out=neg_max[:])
 
         sums = sbuf([P, PASSES], F32, "sums")
         p_turned = []
@@ -139,25 +162,11 @@ def tile_attend_soft_srt_kernel(tc, qT, k_words, k_scales, vT, vs, offs, out):
             )
             p_turned.append(turn_places(p[:], f"turn{g}"))
 
-        v_bf = sbuf([P, PASSES, DV, PACK], BF16, "v_bf")
-
-        def turn_values(picked, turned, g, h):
-            pairs = picked[:, g * PASS : (g + 1) * PASS].bitcast(F32)
-            for u in range(2):
-                nc.tensor.transpose(turned[:, u * P : (u + 1) * P], pairs[:, u : PASS // 2 : 2], ident[:])
-            nc.scalar.copy(
-                v_bf[:, g, h * P : (h + 1) * P, :].bitcast(F32),
-                turned[:, : 2 * P].rearrange("s (u e) -> s e u", u=2),
-            )
-
-        for g in range(PASSES):
-            v0_turned = psum.tile([P, 2 * P], F32, name="v0_turned", tag=f"spare{g}")
-            turn_values(v0_picked, v0_turned[:], g, 0)
-        v1_picked = sbuf([P, N], BF16, "v1_picked", tag="neg_max0")
+        v1_picked = sbuf([P, PASSES, PASS], BF16, "v1_picked", tag="neg_max0")
         v1_turned = psum.tile([P, PASSES, PASS], F32, name="v1_turned", tag="scores")
         for g in range(PASSES):
-            nc.vector.tensor_copy(v1_picked[:, g * PASS : (g + 1) * PASS], v1_pool[:].indirect(slots(g)))
-            turn_values(v1_picked, v1_turned[:, g, :], g, 1)
+            nc.vector.tensor_copy(v1_picked[:, g, :], v1_pool[:].indirect(slots(g)))
+            turn_values(v1_picked[:, g, :], v1_turned[:, g, :], v_bf[1][:, g, :, :])
 
         w_bf = sbuf([P, PASSES, NQ, PACK], BF16, "w_bf", tag="kscale_pool")
         for g in range(PASSES):
@@ -174,16 +183,11 @@ def tile_attend_soft_srt_kernel(tc, qT, k_words, k_scales, vT, vs, offs, out):
             scales=w_scales[:].rearrange("p g q -> p (g q)"),
             in_=w_bf[:].rearrange("p g q t -> p (g q t)"),
         )
-        v_codes = sbuf([P, PASSES, DV], U32, "v_codes")
-        v_scales = sbuf([P, PASSES, DV], U8, "v_scales")
         inv_total = sbuf([P, 1], F32, "inv_total")
         nc.vector.reciprocal(inv_total[:], total[:])
         acc = psum.tile([P, DV], F32, name="acc", tag="spare0")
         for g in range(PASSES):
-            nc.vector.quantize_mx(
-                out=v_codes[:, g, :].bitcast(FP8X4), scales=v_scales[:, g, :],
-                in_=v_bf[:, g, :, :].rearrange("p e t -> p (e t)"),
-            )
+            quantise_values(g, 1)
             nc.tensor.matmul_mx(
                 out=acc[:], lhsT=w_codes[:, g, :].bitcast(FP8X4), lhsT_scale=w_scales[:, g, :],
                 rhs=v_codes[:, g, :].bitcast(FP8X4), rhs_scale=v_scales[:, g, :],

from contextlib import ExitStack

import concourse.mybir as mybir
from concourse.masks import make_identity

N, T, D, DV, NQ = 1024, 4096, 512, 256, 128
FLOPS = 2 * NQ * N * (D + DV)
BYTES = 4 * D * NQ + D * T + (D // 32) * T + 4 * DV * T + 4 * T + 2 * 128 * (N // 16) + 4 * NQ * DV

F32 = mybir.dt.float32
BF16 = mybir.dt.bfloat16
I32 = mybir.dt.int32
U32 = mybir.dt.uint32
U16 = mybir.dt.uint16
U8 = mybir.dt.uint8
FP8X4 = mybir.dt.float8_e4m3fn_x4
ALU = mybir.AluOpType
ACT = mybir.ActivationFunctionType

P = 128
PACK = 4
PASS = P * PACK
PASSES = N // PASS
LIST_COLS = PASS // 16
VS_ROW = 16
ZERO_SPLIT = 3072
PREFIX = T - N + PASS
V0_CHUNKS = ((0, 1024), (1024, 2048), (2048, 2560), (2560, T))


def tile_attend_soft_srt_kernel(tc, qT, k_words, k_scales, vT, vs, offs, out):
    nc = tc.nc
    with ExitStack() as ctx:
        keep = ctx.enter_context(tc.tile_pool(name="keep", bufs=1))
        psum = ctx.enter_context(tc.psum_pool(name="psum", bufs=1))

        def sbuf(shape, dtype, name, tag=None):
            return keep.tile(shape, dtype, name=name, tag=tag or name, align_bytes=64)

        offsets = keep.tile([P, N // 16], U16, name="offsets")
        nc.sync.dma_start(offsets[:], offs)

        def slots(g):
            return offsets[:, g * LIST_COLS : (g + 1) * LIST_COLS]

        q_raw = sbuf([P, PACK, NQ], F32, "q_raw")
        nc.sync.dma_start(q_raw[:], qT[0].rearrange("(p j) q -> p j q", j=PACK))

        def load_v0(i, tag=None):
            c0, c1 = V0_CHUNKS[i]
            chunk = sbuf([P, c1 - c0], F32, f"v0_chunk{i}", tag=tag)
            nc.sync.dma_start(chunk[:], vT[0:P, c0:c1])
            return chunk

        v0_chunks = [load_v0(i) for i in range(len(V0_CHUNKS) - 1)]

        kscale_pool = sbuf([P, T], U8, "kscale_pool")
        nc.gpsimd.memset(kscale_pool[:].bitcast(I32), 0)
        for quad in range(4):
            nc.sync.dma_start(
                kscale_pool[32 * quad : 32 * quad + 4, :].bitcast(I32),
                k_scales[0, 4 * quad : 4 * quad + 4, :].bitcast(I32),
            )
        vs_pool = sbuf([P, T], F32, "vs_pool")
        nc.vector.memset(vs_pool[:, :ZERO_SPLIT].bitcast(I32), 0)
        nc.gpsimd.memset(vs_pool[:, ZERO_SPLIT:].bitcast(I32), 0)
        nc.sync.dma_start(vs_pool[VS_ROW : VS_ROW + 1, :], vs[0:1, :])
        ident = sbuf([P, P], F32, "ident")
        make_identity(nc, ident[:])

        q_bf = sbuf([P, NQ, PACK], BF16, "q_bf")
        nc.scalar.activation(q_bf[:], q_raw[:].rearrange("p j q -> p q j"), ACT.Copy)
        q_codes = sbuf([P, NQ], U32, "q_codes")
        q_scales = sbuf([P, NQ], U8, "q_scales")
        nc.vector.quantize_mx(
            out=q_codes[:].bitcast(FP8X4), scales=q_scales[:], in_=q_bf[:].rearrange("p q j -> p (q j)")
        )

        v0_chunks.append(load_v0(len(V0_CHUNKS) - 1, tag="q_raw"))
        v0_pool_bf = sbuf([P, T], BF16, "v0_pool_bf")
        for (c0, c1), chunk in zip(V0_CHUNKS, v0_chunks):
            nc.scalar.copy(v0_pool_bf[:, c0:c1], chunk[:])

        key_pool = sbuf([P, T], U32, "key_pool", tag="v0_chunk0")
        key_src = k_words[0].rearrange("p n t -> p (n t)").bitcast(I32)
        nc.sync.dma_start(key_pool[:, :PREFIX].bitcast(I32), key_src[:, :PREFIX])
        nc.sync.dma_start(key_pool[:, PREFIX:].bitcast(I32), key_src[:, PREFIX:])

        kscales = sbuf([P, N], U8, "kscales", tag="q_bf")
        nc.vector.tensor_copy(kscales[:], kscale_pool[:].indirect(offsets[:]))

        v1_pool = sbuf([P, T], F32, "v1_pool", tag="kscale_pool")
        nc.sync.dma_start(v1_pool[:], vT[P : 2 * P, :])

        vs_rows = sbuf([P, N], F32, "vs_rows")
        nc.vector.tensor_copy(vs_rows[:], vs_pool[:].indirect(offsets[:]))

        def turn_places(dealt, tag):
            turned = psum.tile([P, PACK, P], F32, name="turned_places", tag=tag)
            for t in range(PACK):
                nc.tensor.transpose(turned[:, t, :], dealt[:, t, :], ident[:])
            return turned

        vs_dealt = sbuf([P, PASSES, PACK, P], F32, "vs_dealt")
        nc.vector.tensor_copy(vs_dealt[:], vs_rows[:].rearrange("m (g s t) -> m g t s", g=PASSES, t=PACK))
        vs_turned = [turn_places(vs_dealt[:, g, :, :], f"spare{g}") for g in range(PASSES)]

        v_bf = [sbuf([P, PASSES, P, PACK], BF16, f"v_bf{h}") for h in range(2)]

        def turn_values(picked, turned, laid):
            pairs = picked.bitcast(F32)
            for u in range(2):
                nc.tensor.transpose(turned[:, u * P : (u + 1) * P], pairs[:, u : PASS // 2 : 2], ident[:])
            nc.scalar.copy(laid.bitcast(F32), turned[:, : 2 * P].rearrange("s (u e) -> s e u", u=2))

        for g in range(PASSES):
            v0_picked = sbuf([P, PASS], BF16, f"v0_picked{g}")
            nc.scalar.activation(v0_picked[:], v0_pool_bf[:].indirect(slots(g)), ACT.Copy)
            v0_turned = psum.tile([P, 2 * P], F32, name="v0_turned", tag=f"turn{g}")
            turn_values(v0_picked[:], v0_turned[:], v_bf[0][:, g, :, :])

        vs_cols = sbuf([P, PASSES, PACK], F32, "vs_cols", tag="v0_pool_bf")
        for g in range(PASSES):
            nc.scalar.copy(vs_cols[:, g, :], vs_turned[g][:, :, VS_ROW])

        keys = sbuf([P, N], U32, "keys", tag="vs_pool")
        scores = psum.tile([P, PASSES, PASS], F32, name="scores", tag="scores")
        for g in range(PASSES):
            cols = slice(g * PASS, (g + 1) * PASS)
            window = key_pool[:, :PREFIX] if g == 0 else key_pool[:]
            nc.vector.tensor_copy(keys[:, cols], window.indirect(slots(g)))
            nc.tensor.matmul_mx(
                out=scores[:, g, :], lhsT=q_codes[:].bitcast(FP8X4), lhsT_scale=q_scales[:],
                rhs=keys[:, cols].bitcast(FP8X4), rhs_scale=kscales[:, cols], start=True, stop=True,
            )
        neg_max0 = sbuf([P, 1], F32, "neg_max0")
        neg_max = sbuf([P, 1], F32, "neg_max")
        neg_scores = sbuf([P, PASS], F32, "neg_scores")
        nc.vector.tensor_reduce(neg_max0[:], scores[:, 0, :], mybir.AxisListType.X, ALU.max, negate=True)

        v_codes = sbuf([P, PASSES, DV], U32, "v_codes", tag="v0_chunk0")
        v_scales = sbuf([P, PASSES, DV], U8, "v_scales")

        def quantise_values(g, h):
            nc.vector.quantize_mx(
                out=v_codes[:, g, h * P : (h + 1) * P].bitcast(FP8X4),
                scales=v_scales[:, g, h * P : (h + 1) * P],
                in_=v_bf[h][:, g, :, :].rearrange("p e t -> p (e t)"),
            )

        for g in range(PASSES):
            quantise_values(g, 0)
        nc.vector.tensor_scalar(neg_scores[:], scores[:, 1, :], -1.0, neg_max0[:], ALU.mult, ALU.min, accum_out=neg_max[:])

        sums = sbuf([P, PASSES], F32, "sums")
        p_turned = []
        for g in range(PASSES):
            p = sbuf([P, PACK, P], F32, f"p{g}")
            nc.scalar.activation(
                p[:], scores[:, g, :].rearrange("q (s t) -> q t s", t=PACK), ACT.Exp,
                bias=neg_max[:], accum_out=sums[:, g : g + 1],
            )
            p_turned.append(turn_places(p[:], f"turn{g}"))

        v1_picked = sbuf([P, PASSES, PASS], BF16, "v1_picked", tag="neg_max0")
        v1_turned = psum.tile([P, PASSES, PASS], F32, name="v1_turned", tag="scores")
        for g in range(PASSES):
            nc.vector.tensor_copy(v1_picked[:, g, :], v1_pool[:].indirect(slots(g)))
            turn_values(v1_picked[:, g, :], v1_turned[:, g, :], v_bf[1][:, g, :, :])

        w_bf = sbuf([P, PASSES, NQ, PACK], BF16, "w_bf", tag="kscale_pool")
        for g in range(PASSES):
            nc.vector.tensor_tensor(
                w_bf[:, g, :, :], p_turned[g][:].rearrange("s t q -> s q t"),
                vs_cols[:, g, :].unsqueeze(1).to_broadcast([P, NQ, PACK]), ALU.mult,
            )
        total = sbuf([P, 1], F32, "total")
        nc.vector.tensor_tensor(total[:], sums[:, 0:1], sums[:, 1:2], ALU.add)
        w_codes = sbuf([P, PASSES, NQ], U32, "w_codes")
        w_scales = sbuf([P, PASSES, NQ], U8, "w_scales")
        nc.vector.quantize_mx(
            out=w_codes[:].rearrange("p g q -> p (g q)").bitcast(FP8X4),
            scales=w_scales[:].rearrange("p g q -> p (g q)"),
            in_=w_bf[:].rearrange("p g q t -> p (g q t)"),
        )
        inv_total = sbuf([P, 1], F32, "inv_total")
        nc.vector.reciprocal(inv_total[:], total[:])
        acc = psum.tile([P, DV], F32, name="acc", tag="spare0")
        for g in range(PASSES):
            quantise_values(g, 1)
            nc.tensor.matmul_mx(
                out=acc[:], lhsT=w_codes[:, g, :].bitcast(FP8X4), lhsT_scale=w_scales[:, g, :],
                rhs=v_codes[:, g, :].bitcast(FP8X4), rhs_scale=v_scales[:, g, :],
                start=(g == 0), stop=(g == PASSES - 1),
            )
        result = sbuf([P, DV], F32, "result")
        nc.vector.tensor_scalar(result[:], acc[:], inv_total[:], None, ALU.mult)
        nc.sync.dma_start(out[0], result[:])
